import numpy as np
import ml_dtypes


def mxq(x, axis, fmt="e4m3"):
    dtype, down = {"e4m3": (ml_dtypes.float8_e4m3fn, 7), "e5m2": (ml_dtypes.float8_e5m2, 14)}[fmt]
    v = np.moveaxis(np.asarray(x, np.float32).astype(ml_dtypes.bfloat16).astype(np.float64), axis, -1)
    blocks = v.reshape(v.shape[:-1] + (-1, 32))
    amax = np.abs(blocks).max(-1, keepdims=True)
    byte = np.maximum(np.where(amax > 0, np.frexp(amax)[1] - 1 + 127, 0) - down, 1)
    scale = np.exp2(byte - 127.0)
    codes = (blocks / scale).astype(np.float32).astype(dtype).astype(np.float64)
    return np.moveaxis((codes * scale).reshape(v.shape), -1, axis)


WIDE = False


def mx_kscale(k):
    if not WIDE:
        return np.ones(k)
    levels = np.array([10, -10, 5, -5, 0])
    if k % 512:
        return np.exp2(np.random.permutation(np.resize(levels, k // 32))).repeat(32)
    a = np.empty((k // 512, 16))
    for p in range(k // 512):
        a[p, :8] = np.random.permutation(np.resize(levels, 8))
        for g in range(8):
            far = levels[np.abs(levels - a[p, g]) >= 10]
            a[p, g + 8] = far[np.random.randint(len(far))]
    return np.exp2(a.ravel()).repeat(32)


def f64(x):
    return np.asarray(x).astype(np.float64)


def striped(idx):
    return np.tile(np.asarray(idx).reshape(-1, 16).T, (8, 1)).astype(np.uint16)


def unstriped(offs):
    return offs[:16].T.reshape(-1).astype(np.int64)


E2M1 = np.array([0.0, 0.5, 1.0, 1.5, 2.0, 3.0, 4.0, 6.0, -0.0, -0.5, -1.0, -1.5, -2.0, -3.0, -4.0, -6.0])


def pack_weight(w, fmt):
    k, n = w.shape
    w = f64(np.asarray(w, np.float32).astype(ml_dtypes.bfloat16)).reshape(k // 32, 32, n)
    amax = np.abs(w).max(1)
    if fmt == "e4m3":
        byte = np.frexp(amax)[1] - 1 + 127 - 7
    else:
        mant, ex = np.frexp(amax / 6.0)
        byte = np.where(mant > 0.5, ex, ex - 1) + 127
    byte = np.clip(np.where(amax > 0, byte, 1), 1, 254)
    scaled = (w * np.exp2(127.0 - byte)[:, None, :]).reshape(k, n).astype(np.float32)
    by_word = np.ascontiguousarray(scaled.reshape(k // 512, 128, 4, n).transpose(0, 1, 3, 2))
    if fmt == "e4m3":
        words = by_word.astype(ml_dtypes.float8_e4m3fn).view(np.uint8)
    else:
        c = by_word.astype(ml_dtypes.float4_e2m1fn).view(np.uint8) & 0xF
        words = (c[..., 0::2] | (c[..., 1::2] << 4)).reshape(k // 512, 128, 2 * n)
    return np.ascontiguousarray(words), np.ascontiguousarray(byte.astype(np.uint8).reshape(k // 512, 16, n))


def unpack_weight(words, scales, fmt):
    g, _, n = scales.shape
    words = np.ascontiguousarray(words).reshape(g, 128, n, -1)
    if fmt == "e4m3":
        vals = words.view(ml_dtypes.float8_e4m3fn).astype(np.float64)
    else:
        nib = np.empty((g, 128, n, 4), np.uint8)
        nib[..., 0::2] = words & 0xF
        nib[..., 1::2] = words >> 4
        vals = E2M1[nib]
    vals = vals * np.repeat(np.exp2(scales.astype(np.float64) - 127.0), 8, axis=1)[..., None]
    return vals.transpose(0, 1, 3, 2).reshape(g * 512, n)


def sigmoid(v):
    return 1.0 / (1.0 + np.exp(-v))


K, R, F, T, J, G = 512, 128, 512, 2048, 512, 64


def setup_inputs():
    n = np.random.standard_normal
    idx = np.random.permutation(T)[:J]
    fk = mx_kscale(K)
    ff = mx_kscale(F)
    tabp = pack_weight(n((K, T)) / fk[:, None], "e4m3")
    dtabp = pack_weight(n((K, T)) / fk[:, None], "e4m3")
    return {
        "tab_words": tabp[0],
        "tab_scales": tabp[1],
        "w1": (n((K, R)) * 1 / np.sqrt(K) * fk[:, None]).astype(np.float32),
        "steep": (np.random.uniform(1.0, 4.0, (R, 1))).astype(np.float32),
        "wo": (n((F, R)) * 1 / np.sqrt(F) * ff[:, None]).astype(np.float32),
        "dy": (n((F, G)) / ff[:, None]).astype(np.float32),
        "dtab_words": dtabp[0],
        "dtab_scales": dtabp[1],
        "og": (np.random.uniform(0.7, 2.0, (R, 1))).astype(np.float32),
        "base": (0.3 * n((R, J))).astype(np.float32),
        "offs": striped(idx),
    }


def reference(tab_words, tab_scales, w1, steep, wo, dy, dtab_words, dtab_scales, og, base, offs):
    idx = unstriped(offs)
    tabu = unpack_weight(tab_words, tab_scales, "e4m3")
    dtabu = unpack_weight(dtab_words, dtab_scales, "e4m3")
    w1q = mxq(f64(w1), 0, "e4m3")
    tabidxg = tabu[:, idx]
    a = w1q.T @ tabidxg
    dtabidxg = dtabu[:, idx]
    ta = w1q.T @ dtabidxg
    h1 = np.tanh(a)
    p = sigmoid(a * f64(steep))
    z = p.reshape(R, G, J // G).sum(axis=2)
    woq = mxq(f64(wo), 0, "e4m3")
    dyq = mxq(f64(dy), 0, "e4m3")
    c0 = woq.T @ dyq
    e1 = c0 / z
    r1 = np.repeat(e1, J // G, axis=1)
    dz = c0 * (p * h1).reshape(R, G, J // G).sum(axis=2) / np.square(z) * (-1.0)
    r2 = np.repeat(dz, J // G, axis=1)
    dp = r1 * h1 + r2
    dh1 = r1 * p
    xh1 = ta * (1.0 - np.square(h1))
    xp = ta * f64(steep) * p * (1.0 - p)
    xz = xp.reshape(R, G, J // G).sum(axis=2)
    xe1 = xz * c0 / np.square(z) * (-1.0)
    xr1 = np.repeat(xe1, J // G, axis=1)
    xdz = ((xp * h1 + xh1 * p).reshape(R, G, J // G).sum(axis=2) * c0 - xz * z * 2.0 * c0 * (p * h1).reshape(R, G, J // G).sum(axis=2) / np.square(z)) / np.square(z) * (-1.0)
    xr2 = np.repeat(xdz, J // G, axis=1)
    xdp = xr1 * h1 + xh1 * r1 + xr2
    xdh1 = xr1 * p + xp * r1
    xda = ((xdp * p + xp * dp) * (1.0 - p) + xp * (-1.0) * dp * p) * f64(steep) + xdh1 * (1.0 - np.square(h1)) + xh1 * h1 * 2.0 * (-1.0) * dh1
    y = xda * f64(og) + f64(base)
    return y

@@ -1,0 +1,190 @@
+from contextlib import ExitStack
+
+import concourse.mybir as mybir
+
+K, R, F, T, J, G = 512, 128, 512, 2048, 512, 64
+FLOPS = 2 * (2 * K * R * J + F * R * G)
+
+F32 = mybir.dt.float32
+BF16 = mybir.dt.bfloat16
+I32 = mybir.dt.int32
+U32 = mybir.dt.uint32
+U16 = mybir.dt.uint16
+U8 = mybir.dt.uint8
+FP8X4 = mybir.dt.float8_e4m3fn_x4
+ACT = mybir.ActivationFunctionType
+ALU = mybir.AluOpType
+AX = mybir.AxisListType
+
+P = 128
+PACK = 4
+GROUP = J // G
+HALVES = 2
+JH = J // HALVES
+GH = G // HALVES
+
+
+def tile_attend_hvgroupvote_kernel(tc, tab_words, tab_scales, w1, steep, wo, dy, dtab_words, dtab_scales, og, base, offs, out):
+    nc = tc.nc
+    with ExitStack() as ctx:
+        keep = ctx.enter_context(tc.tile_pool(name="keep", bufs=1))
+        psum = ctx.enter_context(tc.psum_pool(name="psum", bufs=1))
+
+        offsets = keep.tile([P, J // 16], U16, name="offsets")
+        tw = keep.tile([P, T], U32, name="tw")
+        dw = keep.tile([P, T], U32, name="dw")
+        ts = keep.tile([P, T], U8, name="ts")
+        ds = keep.tile([P, T], U8, name="ds")
+        s_col = keep.tile([P, 1], F32, name="s_col")
+        og_col = keep.tile([P, 1], F32, name="og_col")
+        base_sb = keep.tile([P, J], F32, name="base_sb")
+
+        def load_scales(eng, tile, src):
+            for q in range(4):
+                eng.dma_start(out=tile[32 * q : 32 * q + 4, :].bitcast(I32), in_=src[0, 4 * q : 4 * q + 4, :].bitcast(I32))
+
+        def load_words(tile, src):
+            nc.sync.dma_start(out=tile[:].bitcast(I32), in_=src[0].rearrange("p n t -> p (n t)").bitcast(I32))
+
+        def load_rows(name, src):
+            raw = keep.tile([P, PACK, src.shape[1]], F32, name=name)
+            nc.sync.dma_start(out=raw[:], in_=src.rearrange("(p j) w -> p j w", j=PACK))
+            return raw
+
+        def quantise(name, raw):
+            width = raw.shape[2]
+            grouped = keep.tile([P, width, PACK], BF16, name=name + "_bf", align_bytes=64)
+            codes = keep.tile([P, width], U32, name=name + "_codes", align_bytes=64)
+            scales = keep.tile([P, width], U8, name=name + "_scales", align_bytes=64)
+            nc.scalar.copy(out=grouped[:], in_=raw[:].rearrange("p j w -> p w j"))
+            nc.vector.quantize_mx(out=codes[:].bitcast(FP8X4), scales=scales[:], in_=grouped[:].rearrange("p w j -> p (w j)"))
+            return codes, scales
+
+        nc.vector.memset(ts[:].bitcast(I32), 0)
+        nc.gpsimd.memset(ds[:].bitcast(I32), 0)
+        nc.sync.dma_start(offsets[:], offs)
+        load_scales(nc.scalar, ts, tab_scales)
+        load_words(tw, tab_words)
+        w1_raw = load_rows("w1_raw", w1)
+        nc.sync.dma_start(out=s_col[:], in_=steep)
+        load_scales(nc.sync, ds, dtab_scales)
+        load_words(dw, dtab_words)
+        wo_raw = load_rows("wo_raw", wo)
+        dy_raw = load_rows("dy_raw", dy)
+        nc.sync.dma_start(out=og_col[:], in_=og)
+        nc.sync.dma_start(out=base_sb[:], in_=base)
+
+        def gather(name, window, dtype, hf):
+            picked = keep.tile([P, JH], dtype, name="%s%d" % (name, hf), align_bytes=64)
+            cols = slice(hf * JH // 16, (hf + 1) * JH // 16)
+            nc.vector.tensor_copy(picked[:], window[:].indirect(offsets[:, cols]))
+            return picked
+
+        def product(name, lhs, words, scales):
+            acc = psum.tile([P, words.shape[1]], F32, name=name)
+            nc.tensor.matmul_mx(out=acc[:], lhsT=lhs[0][:].bitcast(FP8X4), lhsT_scale=lhs[1][:],
+                                rhs=words[:].bitcast(FP8X4), rhs_scale=scales[:], start=True, stop=True)
+            return acc
+
+        def wide(name, hf, n=1):
+            return keep.tile([P, n, JH] if n > 1 else [P, JH], F32, name="%s%d" % (name, hf))
+
+        def by_group(ap):
+            return ap.rearrange("p (g i) -> p g i", i=GROUP)
+
+        def spread(ap):
+            return ap.unsqueeze(2).to_broadcast([P, GH, GROUP])
+
+        ts_g = [gather("ts_g", ts, U8, hf) for hf in range(HALVES)]
+        w1_q = quantise("w1", w1_raw)
+        neg = keep.tile([P, 2], F32, name="neg")
+        nc.vector.tensor_scalar(neg[:, 0:1], s_col[:], -1.0, None, ALU.mult)
+        nc.vector.tensor_scalar(neg[:, 1:2], s_col[:], -2.0, None, ALU.mult)
+        a_ps = []
+        for hf in range(HALVES):
+            a_ps.append(product("a%d" % hf, w1_q, gather("tw_g", tw, U32, hf), ts_g[hf]))
+        ds_g = [gather("ds_g", ds, U8, hf) for hf in range(HALVES)]
+
+        st = []
+        for hf in range(HALVES):
+            d = {}
+            d["pp"] = wide("pp", hf, 2)
+            d["h"] = wide("h", hf)
+            d["h2"] = wide("h2", hf)
+            d["v"] = wide("v", hf)
+            d["g"] = wide("g", hf)
+            d["m2"] = wide("m2", hf)
+            p = d["pp"][:, 0, :]
+            nc.scalar.activation(p, a_ps[hf][:], ACT.Sigmoid, scale=s_col[:])
+            nc.scalar.activation(d["h"][:], a_ps[hf][:], ACT.Tanh)
+            nc.scalar.activation(d["v"][:], p, ACT.Identity, bias=s_col[:], scale=neg[:, 0:1])
+            nc.scalar.activation(d["h2"][:], d["h"][:], ACT.Square)
+            nc.scalar.activation(d["m2"][:], d["h"][:], ACT.Identity, bias=neg[:, 0:1], scale=2.0)
+            nc.scalar.activation(d["g"][:], p, ACT.Identity, bias=s_col[:], scale=neg[:, 1:2])
+            st.append(d)
+
+        wo_q = quantise("wo", wo_raw)
+        dy_q = quantise("dy", dy_raw)
+        c0 = product("c0", wo_q, dy_q[0], dy_q[1])
+
+        t_ps = []
+        for hf in range(HALVES):
+            t_ps.append(product("t%d" % hf, w1_q, gather("dw_g", dw, U32, hf), ds_g[hf]))
+
+        for hf in range(HALVES):
+            d = st[hf]
+            p = d["pp"][:, 0, :]
+            d["zs"] = keep.tile([P, 3, GH], F32, name="zs%d" % hf)
+            nc.scalar.activation(d["zs"][:, 2, :], c0[:, hf * GH : (hf + 1) * GH], ACT.Copy, scale=og_col[:])
+            nc.vector.tensor_tensor(d["pp"][:, 1, :], p, d["h"][:], ALU.mult)
+            d["xy"] = wide("xy", hf, 2)
+            nc.vector.tensor_tensor(d["xy"][:, 0, :], p, d["v"][:], ALU.mult)
+            nc.vector.tensor_reduce(d["zs"][:, 0:2, :], d["pp"][:].rearrange("p q (g i) -> p q g i", i=GROUP), AX.X, ALU.add)
+            d["npu"] = wide("npu", hf)
+            nc.vector.scalar_tensor_tensor(d["npu"][:], d["h2"][:], 1.0, p, ALU.subtract, ALU.mult)
+            d["rz"] = keep.tile([P, GH], F32, name="rz%d" % hf)
+            nc.vector.reciprocal(d["rz"][:], d["zs"][:, 0, :])
+            d["pm"] = wide("pm", hf)
+            nc.vector.tensor_tensor(d["pm"][:], d["npu"][:], d["m2"][:], ALU.mult)
+            d["me"] = keep.tile([P, 2, GH], F32, name="me%d" % hf)
+            nc.vector.tensor_tensor(d["me"][:], d["zs"][:, 1:3, :], d["rz"][:].unsqueeze(1).to_broadcast([P, 2, GH]), ALU.mult)
+        for hf in range(HALVES):
+            d = st[hf]
+            d["d"] = wide("d", hf)
+            nc.vector.tensor_tensor(by_group(d["d"][:]), by_group(d["h"][:]), spread(d["me"][:, 0, :]), ALU.subtract)
+            d["te"] = wide("te", hf)
+            nc.vector.tensor_tensor(by_group(d["te"][:]), by_group(t_ps[hf][:]), spread(d["me"][:, 1, :]), ALU.mult)
+        for hf in range(HALVES):
+            d = st[hf]
+            d["xd"] = wide("xd", hf)
+            nc.vector.tensor_tensor(d["xd"][:], d["xy"][:, 0, :], d["d"][:], ALU.mult)
+        for hf in range(HALVES):
+            d = st[hf]
+            nc.vector.tensor_tensor(d["xy"][:, 1, :], d["xd"][:], d["npu"][:], ALU.subtract)
+        for hf in range(HALVES):
+            d = st[hf]
+            d["aa"] = wide("aa", hf, 2)
+            nc.vector.tensor_tensor(d["aa"][:], d["xy"][:], d["te"][:].unsqueeze(1).to_broadcast([P, 2, JH]), ALU.mult)
+        for hf in range(HALVES):
+            d = st[hf]
+            d["sums"] = keep.tile([P, 2, GH], F32, name="sums%d" % hf)
+            nc.vector.tensor_reduce(d["sums"][:], d["aa"][:].rearrange("p q (g i) -> p q g i", i=GROUP), AX.X, ALU.add)
+            d["u1"] = wide("u1", hf)
+            nc.vector.tensor_tensor(d["u1"][:], d["te"][:], d["pm"][:], ALU.mult)
+            d["am"] = keep.tile([P, 2, GH], F32, name="am%d" % hf)
+            nc.vector.tensor_tensor(d["am"][:], d["sums"][:, ::-1, :], d["rz"][:].unsqueeze(1).to_broadcast([P, 2, GH]), ALU.mult)
+            d["u2"] = wide("u2", hf)
+            nc.vector.tensor_tensor(d["u2"][:], d["aa"][:, 1, :], d["g"][:], ALU.mult)
+            d["bb"] = wide("bb", hf, 2)
+            nc.vector.tensor_tensor(d["bb"][:].rearrange("p q (g i) -> p q g i", i=GROUP),
+                                    d["xy"][:].rearrange("p q (g i) -> p q g i", i=GROUP),
+                                    d["am"][:].unsqueeze(3).to_broadcast([P, 2, GH, GROUP]), ALU.mult)
+            d["u3"] = wide("u3", hf)
+            nc.vector.tensor_tensor(d["u3"][:], d["u1"][:], base_sb[:, hf * JH : (hf + 1) * JH], ALU.add)
+            d["u4"] = wide("u4", hf)
+            nc.vector.tensor_tensor(d["u4"][:], d["bb"][:, 0, :], d["bb"][:, 1, :], ALU.add)
+            d["u5"] = wide("u5", hf)
+            nc.vector.tensor_tensor(d["u5"][:], d["u3"][:], d["u2"][:], ALU.add)
+            d["y"] = wide("y", hf)
+            nc.vector.tensor_tensor(d["y"][:], d["u5"][:], d["u4"][:], ALU.subtract)
+            nc.sync.dma_start(out=out[:, hf * JH : (hf + 1) * JH], in_=d["y"][:])

@@ -1,6 +1,7 @@
 from contextlib import ExitStack
 
 import concourse.mybir as mybir
+from concourse.masks import make_identity
 
 K, R, F, T, J, G = 512, 128, 512, 2048, 512, 64
 FLOPS = 2 * (2 * K * R * J + F * R * G)
@@ -22,6 +23,8 @@ GROUP = J // G
 HALVES = 2
 JH = J // HALVES
 GH = G // HALVES
+PAIRS = GROUP // 2
+RUN = 2 * GH
 
 
 def tile_attend_hvgroupvote_kernel(tc, tab_words, tab_scales, w1, steep, wo, dy, dtab_words, dtab_scales, og, base, offs, out):
@@ -32,28 +35,24 @@ def tile_attend_hvgroupvote_kernel(tc, tab_words, tab_scales, w1, steep, wo, dy,
 
         offsets = keep.tile([P, J // 16], U16, name="offsets")
         tw = keep.tile([P, T], U32, name="tw")
-        dw = keep.tile([P, T], U32, name="dw")
-        ts = keep.tile([P, T], U8, name="ts")
-        ds = keep.tile([P, T], U8, name="ds")
+        ts = keep.tile([P, T], U8, name="ts", tag="ts")
         s_col = keep.tile([P, 1], F32, name="s_col")
-        og_col = keep.tile([P, 1], F32, name="og_col")
-        base_sb = keep.tile([P, J], F32, name="base_sb")
 
         def load_scales(eng, tile, src):
             for q in range(4):
                 eng.dma_start(out=tile[32 * q : 32 * q + 4, :].bitcast(I32), in_=src[0, 4 * q : 4 * q + 4, :].bitcast(I32))
 
-        def load_words(tile, src):
-            nc.sync.dma_start(out=tile[:].bitcast(I32), in_=src[0].rearrange("p n t -> p (n t)").bitcast(I32))
+        def load_words(eng, tile, src):
+            eng.dma_start(out=tile[:].bitcast(I32), in_=src[0].rearrange("p n t -> p (n t)").bitcast(I32))
 
         def load_rows(name, src):
-            raw = keep.tile([P, PACK, src.shape[1]], F32, name=name)
+            raw = keep.tile([P, PACK, src.shape[1]], F32, name=name, tag=name)
             nc.sync.dma_start(out=raw[:], in_=src.rearrange("(p j) w -> p j w", j=PACK))
             return raw
 
         def quantise(name, raw):
             width = raw.shape[2]
-            grouped = keep.tile([P, width, PACK], BF16, name=name + "_bf", align_bytes=64)
+            grouped = keep.tile([P, width, PACK], BF16, name=name + "_bf", tag=name + "_bf", align_bytes=64)
             codes = keep.tile([P, width], U32, name=name + "_codes", align_bytes=64)
             scales = keep.tile([P, width], U8, name=name + "_scales", align_bytes=64)
             nc.scalar.copy(out=grouped[:], in_=raw[:].rearrange("p j w -> p w j"))
@@ -61,130 +60,285 @@ def tile_attend_hvgroupvote_kernel(tc, tab_words, tab_scales, w1, steep, wo, dy,
             return codes, scales
 
         nc.vector.memset(ts[:].bitcast(I32), 0)
+        warm = keep.tile([P, 1], F32, name="warm")
+        nc.gpsimd.memset(warm[:], 0.0)
+        nc.scalar.activation(warm[:], warm[:], ACT.Sigmoid)
+        ds = keep.tile([P, T], U8, name="ds")
         nc.gpsimd.memset(ds[:].bitcast(I32), 0)
+        ident = keep.tile([P, P], F32, name="ident")
+        make_identity(nc, ident[:])
         nc.sync.dma_start(offsets[:], offs)
-        load_scales(nc.scalar, ts, tab_scales)
-        load_words(tw, tab_words)
         w1_raw = load_rows("w1_raw", w1)
+        load_scales(nc.sync, ts, tab_scales)
+        load_words(nc.sync, tw, tab_words)
         nc.sync.dma_start(out=s_col[:], in_=steep)
         load_scales(nc.sync, ds, dtab_scales)
-        load_words(dw, dtab_words)
         wo_raw = load_rows("wo_raw", wo)
         dy_raw = load_rows("dy_raw", dy)
-        nc.sync.dma_start(out=og_col[:], in_=og)
-        nc.sync.dma_start(out=base_sb[:], in_=base)
 
         def gather(name, window, dtype, hf):
-            picked = keep.tile([P, JH], dtype, name="%s%d" % (name, hf), align_bytes=64)
+            picked = keep.tile([P, JH], dtype, name="%s%d" % (name, hf), tag="picked_%s%d" % (name[1], hf), align_bytes=64)
             cols = slice(hf * JH // 16, (hf + 1) * JH // 16)
             nc.vector.tensor_copy(picked[:], window[:].indirect(offsets[:, cols]))
             return picked
 
         def product(name, lhs, words, scales):
-            acc = psum.tile([P, words.shape[1]], F32, name=name)
+            acc = psum.tile([P, words.shape[1]], F32, name=name, tag=name)
             nc.tensor.matmul_mx(out=acc[:], lhsT=lhs[0][:].bitcast(FP8X4), lhsT_scale=lhs[1][:],
                                 rhs=words[:].bitcast(FP8X4), rhs_scale=scales[:], start=True, stop=True)
             return acc
 
-        def wide(name, hf, n=1):
-            return keep.tile([P, n, JH] if n > 1 else [P, JH], F32, name="%s%d" % (name, hf))
+        def wide(name, hf):
+            return keep.tile([P, PAIRS, RUN], F32, name="%s%d" % (name, hf))
 
-        def by_group(ap):
-            return ap.rearrange("p (g i) -> p g i", i=GROUP)
+        def stack(name, hf):
+            return keep.tile([P, PAIRS, 2, RUN], F32, name="%s%d" % (name, hf))
+
+        def dealt(ap):
+            return ap.rearrange("p (g i e) -> p i g e", i=PAIRS, e=2)
+
+        def split(ap):
+            return ap.rearrange("p i (g e) -> p i g e", e=2)
 
         def spread(ap):
-            return ap.unsqueeze(2).to_broadcast([P, GH, GROUP])
+            n = ap.shape[1]
+            return ap.unsqueeze(1).unsqueeze(3).to_broadcast([P, PAIRS, n, 2])
+
+        def turn_sums(name, hf, both):
+            bank = psum.tile([P, 2, P], F32, name=name, tag="sum%d" % hf)
+            for i in range(PAIRS):
+                nc.tensor.matmul(bank[:, 0, :], lhsT=both[:, i, :, :].rearrange("p q x -> p (q x)"), rhs=ident[:],
+                                 start=(i == 0), stop=(i == PAIRS - 1), is_transpose=True)
+            return bank
+
+        def turn_back(name, bank):
+            turned = keep.tile([P, P], F32, name=name + "_turned", tag=name + "_turned", align_bytes=64)
+            nc.scalar.copy(out=turned[:], in_=bank[:, 0, :])
+            pairs = bank[:, 1, :].rearrange("p (x e) -> p x e", e=2)
+            nc.tensor.matmul(pairs, lhsT=turned[:], rhs=ident[:], start=True, stop=False, is_transpose=True)
+            nc.tensor.matmul(pairs[:, :, ::-1], lhsT=turned[:], rhs=ident[:], start=False, stop=True, is_transpose=True)
+            return pairs[:, :, 0].rearrange("p (q g) -> p q g", q=2)
 
         ts_g = [gather("ts_g", ts, U8, hf) for hf in range(HALVES)]
         w1_q = quantise("w1", w1_raw)
-        neg = keep.tile([P, 2], F32, name="neg")
-        nc.vector.tensor_scalar(neg[:, 0:1], s_col[:], -1.0, None, ALU.mult)
-        nc.vector.tensor_scalar(neg[:, 1:2], s_col[:], -2.0, None, ALU.mult)
+        dw = keep.tile([P, T], U32, name="dw", tag="ts")
+        load_words(nc.scalar, dw, dtab_words)
+        neg_s = keep.tile([P, 1], F32, name="neg_s")
+        half_s = keep.tile([P, 1], F32, name="half_s")
+        nc.gpsimd.tensor_scalar(neg_s[:], s_col[:], -1.0, 0.0, ALU.mult, ALU.add)
+        nc.gpsimd.tensor_scalar(half_s[:], s_col[:], 0.5, 0.0, ALU.mult, ALU.add)
         a_ps = []
         for hf in range(HALVES):
             a_ps.append(product("a%d" % hf, w1_q, gather("tw_g", tw, U32, hf), ts_g[hf]))
-        ds_g = [gather("ds_g", ds, U8, hf) for hf in range(HALVES)]
 
-        st = []
+        st = [dict() for hf in range(HALVES)]
         for hf in range(HALVES):
-            d = {}
-            d["pp"] = wide("pp", hf, 2)
-            d["h"] = wide("h", hf)
-            d["h2"] = wide("h2", hf)
-            d["v"] = wide("v", hf)
-            d["g"] = wide("g", hf)
-            d["m2"] = wide("m2", hf)
-            p = d["pp"][:, 0, :]
-            nc.scalar.activation(p, a_ps[hf][:], ACT.Sigmoid, scale=s_col[:])
-            nc.scalar.activation(d["h"][:], a_ps[hf][:], ACT.Tanh)
-            nc.scalar.activation(d["v"][:], p, ACT.Identity, bias=s_col[:], scale=neg[:, 0:1])
+            d = st[hf]
+            for name in ("h", "h2", "pn", "tn", "m2", "npu", "te", "u1", "u2"):
+                d[name] = wide(name, hf)
+            for name in ("pp", "xy", "aa"):
+                d[name] = stack(name, hf)
+            d["bb"] = keep.tile([P, 2, PAIRS, RUN], F32, name="bb%d" % hf)
+            for name in ("am",):
+                d[name] = keep.tile([P, 2, GH], F32, name="%s%d" % (name, hf))
+            for name in ("m", "e"):
+                d[name] = keep.tile([P, GH], F32, name="%s%d" % (name, hf))
+            d["p"] = d["pp"][:, :, 0, :]
+            d["a"] = dealt(a_ps[hf][:])
+
+        def s_ph(hf):
+            d = st[hf]
+            nc.scalar.activation(split(d["p"]), d["a"], ACT.Sigmoid, scale=s_col[:])
+            nc.scalar.activation(split(d["h"][:]), d["a"], ACT.Tanh)
+
+        def s_pn_h2(hf):
+            d = st[hf]
+            nc.scalar.activation(split(d["pn"][:]), d["a"], ACT.Sigmoid, scale=neg_s[:])
             nc.scalar.activation(d["h2"][:], d["h"][:], ACT.Square)
-            nc.scalar.activation(d["m2"][:], d["h"][:], ACT.Identity, bias=neg[:, 0:1], scale=2.0)
-            nc.scalar.activation(d["g"][:], p, ACT.Identity, bias=s_col[:], scale=neg[:, 1:2])
-            st.append(d)
+
+        def s_rest(hf):
+            d = st[hf]
+            nc.scalar.activation(d["m2"][:], d["h"][:], ACT.Identity, bias=neg_s[:], scale=2.0)
+            nc.scalar.activation(split(d["tn"][:]), d["a"], ACT.Tanh, scale=half_s[:])
+
+        def s_base(hf):
+            st[hf]["bs"] = keep.tile([P, PAIRS, RUN], F32, name="bs%d" % hf, tag="zs_ps%d_turned" % hf, align_bytes=64)
+            nc.scalar.copy(out=split(st[hf]["bs"][:]), in_=dealt(base_sb[:, hf * JH : (hf + 1) * JH]))
+
+        def v_ph(hf):
+            d = st[hf]
+            nc.vector.tensor_tensor(d["pp"][:, :, 1, :], d["p"], d["h"][:], ALU.mult)
+            d["zs_ps"] = turn_sums("zs_ps%d" % hf, hf, d["pp"])
+
+        def back_zs(hf):
+            st[hf]["zs"] = turn_back("zs_ps%d" % hf, st[hf]["zs_ps"])
+
+        def back_aa(hf):
+            st[hf]["sums"] = turn_back("aa_ps%d" % hf, st[hf]["aa_ps"])
+
+        def v_rz(hf):
+            d = st[hf]
+            d["rz"] = keep.tile([P, GH], F32, name="rz%d" % hf, tag=("rz0", "d0")[hf])
+            nc.vector.reciprocal(d["rz"][:], d["zs"][:, 0, :])
+
+        def v_m(hf):
+            d = st[hf]
+            nc.vector.tensor_tensor(d["m"][:], d["zs"][:, 1, :], d["rz"][:], ALU.mult)
+
+        def v_x(hf):
+            d = st[hf]
+            nc.vector.scalar_tensor_tensor(d["xy"][:, :, 0, :], d["p"], s_col[:], d["pn"][:], ALU.mult, ALU.mult)
+
+        def v_npu(hf):
+            d = st[hf]
+            nc.vector.scalar_tensor_tensor(d["npu"][:], d["h2"][:], 1.0, d["p"], ALU.subtract, ALU.mult)
+
+        def v_d(hf):
+            d = st[hf]
+            d["d"] = keep.tile([P, PAIRS, RUN], F32, name="d%d" % hf, tag="d%d" % hf)
+            nc.vector.tensor_tensor(split(d["d"][:]), split(d["h"][:]), spread(d["m"][:]), ALU.subtract)
+
+        def v_xd(hf):
+            d = st[hf]
+            d["xd"] = keep.tile([P, PAIRS, RUN], F32, name="xd%d" % hf, tag="xd%d" % hf)
+            nc.vector.tensor_tensor(d["xd"][:], d["xy"][:, :, 0, :], d["d"][:], ALU.mult)
+
+        def v_y(hf):
+            d = st[hf]
+            nc.vector.tensor_tensor(d["xy"][:, :, 1, :], d["xd"][:], d["npu"][:], ALU.subtract)
+
+        def v_ds(hf):
+            st[hf]["ds_g"] = gather("ds_g", ds, U8, hf)
+
+        def v_dw(hf):
+            st[hf]["t"] = product("t%d" % hf, w1_q, gather("dw_g", dw, U32, hf), st[hf]["ds_g"])
+
+        def v_e(hf):
+            d = st[hf]
+            nc.vector.scalar_tensor_tensor(d["e"][:], c0[:, hf * GH : (hf + 1) * GH], og_col[:], d["rz"][:], ALU.mult, ALU.mult)
+
+        def v_te(hf):
+            d = st[hf]
+            nc.vector.tensor_tensor(split(d["te"][:]), dealt(d["t"][:]), spread(d["e"][:]), ALU.mult)
+
+        def v_aa(hf):
+            d = st[hf]
+            nc.vector.tensor_tensor(d["aa"][:], d["xy"][:], d["te"][:].unsqueeze(2).to_broadcast([P, PAIRS, 2, RUN]), ALU.mult)
+
+        def pe_sums(hf):
+            st[hf]["aa_ps"] = turn_sums("aa_ps%d" % hf, hf, st[hf]["aa"])
+
+        def v_sums(hf):
+            d = st[hf]
+            sums = keep.tile([P, 2 * GH], F32, name="sums%d" % hf)
+            nc.vector.tensor_reduce(sums[:], d["aa"][:].rearrange("p i q (g e) -> p (q g) i e", e=2), AX.XY, ALU.add)
+            d["sums"] = sums[:].rearrange("p (q g) -> p q g", q=2)
+
+        def v_am(hf):
+            d = st[hf]
+            nc.vector.scalar_tensor_tensor(d["am"][:], d["sums"][:, ::-1, :], -1.0,
+                                           d["rz"][:].unsqueeze(1).to_broadcast([P, 2, GH]), ALU.mult, ALU.mult)
+
+        def v_pm(hf):
+            d = st[hf]
+            d["pm"] = keep.tile([P, PAIRS, RUN], F32, name="pm%d" % hf, tag=("xd1", "d1")[hf])
+            nc.vector.tensor_tensor(d["pm"][:], d["npu"][:], d["m2"][:], ALU.mult)
+
+        def v_u1(hf):
+            d = st[hf]
+            nc.vector.tensor_tensor(d["u1"][:], d["te"][:], d["pm"][:], ALU.mult)
+
+        def v_u2(hf):
+            d = st[hf]
+            nc.vector.scalar_tensor_tensor(d["u2"][:], d["aa"][:, :, 1, :], neg_s[:], d["tn"][:], ALU.mult, ALU.mult)
+
+        def v_bb(hf):
+            d = st[hf]
+            for q in range(2):
+                nc.vector.tensor_tensor(split(d["bb"][:, q, :, :]), split(d["xy"][:, :, q, :]), spread(d["am"][:, q, :]), ALU.mult)
+
+        def add_terms(hf, terms, tags):
+            banks = [psum.tile([P, P], F32, name="u_ps%d%d" % (hf, c), tag=tags[c]) for c in range(2)]
+            for n, term in enumerate(terms):
+                for c in range(2):
+                    nc.tensor.matmul(banks[c][:], lhsT=term[:, 2 * c : 2 * c + 2, :].rearrange("p i x -> p (i x)"), rhs=ident[:],
+                                     start=(n == 0), stop=(n == len(terms) - 1), is_transpose=True)
+            back = psum.tile([P, 2, P], F32, name="u_back%d" % hf, tag=tags[2])
+            for c in range(2):
+                turned = keep.tile([P, P], F32, name="u_turned%d%d" % (hf, c))
+                nc.scalar.copy(out=turned[:], in_=banks[c][:])
+                nc.tensor.transpose(back[:, c, :], turned[:], ident[:])
+            return back[:].rearrange("p c (j g e) -> p g (c j) e", j=2, e=2)
+
+        def store(hf, y):
+            nc.sync.dma_start(out=out[:, hf * JH : (hf + 1) * JH], in_=y[:].rearrange("p g i e -> p (g i e)"))
 
         wo_q = quantise("wo", wo_raw)
+        base_sb = keep.tile([P, J], F32, name="base_sb", tag="wo_raw")
+        nc.sync.dma_start(out=base_sb[:], in_=base)
         dy_q = quantise("dy", dy_raw)
+        og_col = keep.tile([P, 1], F32, name="og_col", tag="dy_raw")
+        nc.sync.dma_start(out=og_col[:], in_=og)
         c0 = product("c0", wo_q, dy_q[0], dy_q[1])
-
-        t_ps = []
-        for hf in range(HALVES):
-            t_ps.append(product("t%d" % hf, w1_q, gather("dw_g", dw, U32, hf), ds_g[hf]))
-
-        for hf in range(HALVES):
-            d = st[hf]
-            p = d["pp"][:, 0, :]
-            d["zs"] = keep.tile([P, 3, GH], F32, name="zs%d" % hf)
-            nc.scalar.activation(d["zs"][:, 2, :], c0[:, hf * GH : (hf + 1) * GH], ACT.Copy, scale=og_col[:])
-            nc.vector.tensor_tensor(d["pp"][:, 1, :], p, d["h"][:], ALU.mult)
-            d["xy"] = wide("xy", hf, 2)
-            nc.vector.tensor_tensor(d["xy"][:, 0, :], p, d["v"][:], ALU.mult)
-            nc.vector.tensor_reduce(d["zs"][:, 0:2, :], d["pp"][:].rearrange("p q (g i) -> p q g i", i=GROUP), AX.X, ALU.add)
-            d["npu"] = wide("npu", hf)
-            nc.vector.scalar_tensor_tensor(d["npu"][:], d["h2"][:], 1.0, p, ALU.subtract, ALU.mult)
-            d["rz"] = keep.tile([P, GH], F32, name="rz%d" % hf)
-            nc.vector.reciprocal(d["rz"][:], d["zs"][:, 0, :])
-            d["pm"] = wide("pm", hf)
-            nc.vector.tensor_tensor(d["pm"][:], d["npu"][:], d["m2"][:], ALU.mult)
-            d["me"] = keep.tile([P, 2, GH], F32, name="me%d" % hf)
-            nc.vector.tensor_tensor(d["me"][:], d["zs"][:, 1:3, :], d["rz"][:].unsqueeze(1).to_broadcast([P, 2, GH]), ALU.mult)
-        for hf in range(HALVES):
-            d = st[hf]
-            d["d"] = wide("d", hf)
-            nc.vector.tensor_tensor(by_group(d["d"][:]), by_group(d["h"][:]), spread(d["me"][:, 0, :]), ALU.subtract)
-            d["te"] = wide("te", hf)
-            nc.vector.tensor_tensor(by_group(d["te"][:]), by_group(t_ps[hf][:]), spread(d["me"][:, 1, :]), ALU.mult)
-        for hf in range(HALVES):
-            d = st[hf]
-            d["xd"] = wide("xd", hf)
-            nc.vector.tensor_tensor(d["xd"][:], d["xy"][:, 0, :], d["d"][:], ALU.mult)
-        for hf in range(HALVES):
-            d = st[hf]
-            nc.vector.tensor_tensor(d["xy"][:, 1, :], d["xd"][:], d["npu"][:], ALU.subtract)
-        for hf in range(HALVES):
-            d = st[hf]
-            d["aa"] = wide("aa", hf, 2)
-            nc.vector.tensor_tensor(d["aa"][:], d["xy"][:], d["te"][:].unsqueeze(1).to_broadcast([P, 2, JH]), ALU.mult)
-        for hf in range(HALVES):
-            d = st[hf]
-            d["sums"] = keep.tile([P, 2, GH], F32, name="sums%d" % hf)
-            nc.vector.tensor_reduce(d["sums"][:], d["aa"][:].rearrange("p q (g i) -> p q g i", i=GROUP), AX.X, ALU.add)
-            d["u1"] = wide("u1", hf)
-            nc.vector.tensor_tensor(d["u1"][:], d["te"][:], d["pm"][:], ALU.mult)
-            d["am"] = keep.tile([P, 2, GH], F32, name="am%d" % hf)
-            nc.vector.tensor_tensor(d["am"][:], d["sums"][:, ::-1, :], d["rz"][:].unsqueeze(1).to_broadcast([P, 2, GH]), ALU.mult)
-            d["u2"] = wide("u2", hf)
-            nc.vector.tensor_tensor(d["u2"][:], d["aa"][:, 1, :], d["g"][:], ALU.mult)
-            d["bb"] = wide("bb", hf, 2)
-            nc.vector.tensor_tensor(d["bb"][:].rearrange("p q (g i) -> p q g i", i=GROUP),
-                                    d["xy"][:].rearrange("p q (g i) -> p q g i", i=GROUP),
-                                    d["am"][:].unsqueeze(3).to_broadcast([P, 2, GH, GROUP]), ALU.mult)
-            d["u3"] = wide("u3", hf)
-            nc.vector.tensor_tensor(d["u3"][:], d["u1"][:], base_sb[:, hf * JH : (hf + 1) * JH], ALU.add)
-            d["u4"] = wide("u4", hf)
-            nc.vector.tensor_tensor(d["u4"][:], d["bb"][:, 0, :], d["bb"][:, 1, :], ALU.add)
-            d["u5"] = wide("u5", hf)
-            nc.vector.tensor_tensor(d["u5"][:], d["u3"][:], d["u2"][:], ALU.add)
-            d["y"] = wide("y", hf)
-            nc.vector.tensor_tensor(d["y"][:], d["u5"][:], d["u4"][:], ALU.subtract)
-            nc.sync.dma_start(out=out[:, hf * JH : (hf + 1) * JH], in_=d["y"][:])
+        s_ph(0)
+        s_ph(1)
+        v_ds(0)
+        v_ds(1)
+        v_ph(0)
+        v_ph(1)
+        s_pn_h2(0)
+        back_zs(0)
+        s_pn_h2(1)
+        back_zs(1)
+        v_x(0)
+        v_npu(0)
+        v_dw(0)
+        v_dw(1)
+        v_x(1)
+        v_npu(1)
+        v_rz(0)
+        s_rest(0)
+        s_rest(1)
+        s_base(0)
+        s_base(1)
+        v_m(0)
+        v_e(0)
+        v_d(0)
+        v_te(0)
+        v_xd(0)
+        v_rz(1)
+        v_y(0)
+        v_m(1)
+        v_aa(0)
+        pe_sums(0)
+        back_aa(0)
+        v_d(1)
+        v_e(1)
+        v_xd(1)
+        v_te(1)
+        v_y(1)
+        v_pm(0)
+        v_u2(0)
+        v_u1(0)
+        v_am(0)
+        v_pm(1)
+        v_bb(0)
+        d = st[0]
+        whole0 = add_terms(0, (d["bs"], d["u1"], d["u2"], d["bb"][:, 0, :, :], d["bb"][:, 1, :, :]), ("a0", "t0", "spare"))
+        y0 = keep.tile([P, GH, PAIRS, 2], F32, name="y0")
+        nc.scalar.copy(out=y0[:], in_=whole0)
+        store(0, y0)
+        v_u1(1)
+        v_aa(1)
+        v_u2(1)
+        d = st[1]
+        part1 = add_terms(1, (d["bs"], d["u1"], d["u2"]), ("a1", "t1", "c0"))
+        v_sums(1)
+        v_am(1)
+        v_bb(1)
+        d = st[1]
+        u4 = wide("u4", 1)
+        nc.vector.tensor_tensor(u4[:], d["bb"][:, 0, :, :], d["bb"][:, 1, :, :], ALU.add)
+        y1 = keep.tile([P, GH, PAIRS, 2], F32, name="y1")
+        nc.vector.tensor_tensor(y1[:], part1, u4[:].rearrange("p i (g e) -> p g i e", e=2), ALU.add)
+        store(1, y1)

from contextlib import ExitStack

import concourse.mybir as mybir
from concourse.masks import make_identity

K, R, F, T, J, G = 512, 128, 512, 2048, 512, 64
FLOPS = 2 * (2 * K * R * J + F * R * G)

F32 = mybir.dt.float32
BF16 = mybir.dt.bfloat16
I32 = mybir.dt.int32
U32 = mybir.dt.uint32
U16 = mybir.dt.uint16
U8 = mybir.dt.uint8
FP8X4 = mybir.dt.float8_e4m3fn_x4
ACT = mybir.ActivationFunctionType
ALU = mybir.AluOpType
AX = mybir.AxisListType

P = 128
PACK = 4
GROUP = J // G
HALVES = 2
JH = J // HALVES
GH = G // HALVES
PAIRS = GROUP // 2
RUN = 2 * GH


def tile_attend_hvgroupvote_kernel(tc, tab_words, tab_scales, w1, steep, wo, dy, dtab_words, dtab_scales, og, base, offs, out):
    nc = tc.nc
    with ExitStack() as ctx:
        keep = ctx.enter_context(tc.tile_pool(name="keep", bufs=1))
        psum = ctx.enter_context(tc.psum_pool(name="psum", bufs=1))

        offsets = keep.tile([P, J // 16], U16, name="offsets")
        tw = keep.tile([P, T], U32, name="tw")
        ts = keep.tile([P, T], U8, name="ts", tag="ts")
        s_col = keep.tile([P, 1], F32, name="s_col")

        def load_scales(eng, tile, src):
            for q in range(4):
                eng.dma_start(out=tile[32 * q : 32 * q + 4, :].bitcast(I32), in_=src[0, 4 * q : 4 * q + 4, :].bitcast(I32))

        def load_words(eng, tile, src):
            eng.dma_start(out=tile[:].bitcast(I32), in_=src[0].rearrange("p n t -> p (n t)").bitcast(I32))

        def load_rows(name, src):
            raw = keep.tile([P, PACK, src.shape[1]], F32, name=name, tag=name)
            nc.sync.dma_start(out=raw[:], in_=src.rearrange("(p j) w -> p j w", j=PACK))
            return raw

        def quantise(name, raw):
            width = raw.shape[2]
            grouped = keep.tile([P, width, PACK], BF16, name=name + "_bf", tag=name + "_bf", align_bytes=64)
            codes = keep.tile([P, width], U32, name=name + "_codes", align_bytes=64)
            scales = keep.tile([P, width], U8, name=name + "_scales", align_bytes=64)
            nc.scalar.copy(out=grouped[:], in_=raw[:].rearrange("p j w -> p w j"))
            nc.vector.quantize_mx(out=codes[:].bitcast(FP8X4), scales=scales[:], in_=grouped[:].rearrange("p w j -> p (w j)"))
            return codes, scales

        nc.vector.memset(ts[:].bitcast(I32), 0)
        warm = keep.tile([P, 1], F32, name="warm")
        nc.gpsimd.memset(warm[:], 0.0)
        nc.scalar.activation(warm[:], warm[:], ACT.Sigmoid)
        ds = keep.tile([P, T], U8, name="ds")
        nc.gpsimd.memset(ds[:].bitcast(I32), 0)
        ident = keep.tile([P, P], F32, name="ident")
        make_identity(nc, ident[:])
        nc.sync.dma_start(offsets[:], offs)
        w1_raw = load_rows("w1_raw", w1)
        load_scales(nc.sync, ts, tab_scales)
        load_words(nc.sync, tw, tab_words)
        nc.sync.dma_start(out=s_col[:], in_=steep)
        load_scales(nc.sync, ds, dtab_scales)
        wo_raw = load_rows("wo_raw", wo)
        dy_raw = load_rows("dy_raw", dy)

        def gather(name, window, dtype, hf):
            picked = keep.tile([P, JH], dtype, name="%s%d" % (name, hf), tag="picked_%s%d" % (name[1], hf), align_bytes=64)
            cols = slice(hf * JH // 16, (hf + 1) * JH // 16)
            nc.vector.tensor_copy(picked[:], window[:].indirect(offsets[:, cols]))
            return picked

        def product(name, lhs, words, scales):
            acc = psum.tile([P, words.shape[1]], F32, name=name, tag=name)
            nc.tensor.matmul_mx(out=acc[:], lhsT=lhs[0][:].bitcast(FP8X4), lhsT_scale=lhs[1][:],
                                rhs=words[:].bitcast(FP8X4), rhs_scale=scales[:], start=True, stop=True)
            return acc

        def wide(name, hf):
            return keep.tile([P, PAIRS, RUN], F32, name="%s%d" % (name, hf))

        def stack(name, hf):
            return keep.tile([P, PAIRS, 2, RUN], F32, name="%s%d" % (name, hf))

        def dealt(ap):
            return ap.rearrange("p (g i e) -> p i g e", i=PAIRS, e=2)

        def split(ap):
            return ap.rearrange("p i (g e) -> p i g e", e=2)

        def spread(ap):
            n = ap.shape[1]
            return ap.unsqueeze(1).unsqueeze(3).to_broadcast([P, PAIRS, n, 2])

        def turn_sums(name, hf, both):
            bank = psum.tile([P, 2, P], F32, name=name, tag="sum%d" % hf)
            for i in range(PAIRS):
                nc.tensor.matmul(bank[:, 0, :], lhsT=both[:, i, :, :].rearrange("p q x -> p (q x)"), rhs=ident[:],
                                 start=(i == 0), stop=(i == PAIRS - 1), is_transpose=True)
            return bank

        def turn_back(name, bank):
            turned = keep.tile([P, P], F32, name=name + "_turned", tag=name + "_turned", align_bytes=64)
            nc.scalar.copy(out=turned[:], in_=bank[:, 0, :])
            pairs = bank[:, 1, :].rearrange("p (x e) -> p x e", e=2)
            nc.tensor.matmul(pairs, lhsT=turned[:], rhs=ident[:], start=True, stop=False, is_transpose=True)
            nc.tensor.matmul(pairs[:, :, ::-1], lhsT=turned[:], rhs=ident[:], start=False, stop=True, is_transpose=True)
            return pairs[:, :, 0].rearrange("p (q g) -> p q g", q=2)

        ts_g = [gather("ts_g", ts, U8, hf) for hf in range(HALVES)]
        w1_q = quantise("w1", w1_raw)
        dw = keep.tile([P, T], U32, name="dw", tag="ts")
        load_words(nc.scalar, dw, dtab_words)
        neg_s = keep.tile([P, 1], F32, name="neg_s")
        half_s = keep.tile([P, 1], F32, name="half_s")
        nc.gpsimd.tensor_scalar(neg_s[:], s_col[:], -1.0, 0.0, ALU.mult, ALU.add)
        nc.gpsimd.tensor_scalar(half_s[:], s_col[:], 0.5, 0.0, ALU.mult, ALU.add)
        a_ps = []
        for hf in range(HALVES):
            a_ps.append(product("a%d" % hf, w1_q, gather("tw_g", tw, U32, hf), ts_g[hf]))

        st = [dict() for hf in range(HALVES)]
        for hf in range(HALVES):
            d = st[hf]
            for name in ("h", "h2", "pn", "tn", "m2", "npu", "te", "u1", "u2"):
                d[name] = wide(name, hf)
            for name in ("pp", "xy", "aa"):
                d[name] = stack(name, hf)
            d["bb"] = keep.tile([P, 2, PAIRS, RUN], F32, name="bb%d" % hf)
            for name in ("am",):
                d[name] = keep.tile([P, 2, GH], F32, name="%s%d" % (name, hf))
            for name in ("m", "e"):
                d[name] = keep.tile([P, GH], F32, name="%s%d" % (name, hf))
            d["p"] = d["pp"][:, :, 0, :]
            d["a"] = dealt(a_ps[hf][:])

        def s_ph(hf):
            d = st[hf]
            nc.scalar.activation(split(d["p"]), d["a"], ACT.Sigmoid, scale=s_col[:])
            nc.scalar.activation(split(d["h"][:]), d["a"], ACT.Tanh)

        def s_pn_h2(hf):
            d = st[hf]
            nc.scalar.activation(split(d["pn"][:]), d["a"], ACT.Sigmoid, scale=neg_s[:])
            nc.scalar.activation(d["h2"][:], d["h"][:], ACT.Square)

        def s_rest(hf):
            d = st[hf]
            nc.scalar.activation(d["m2"][:], d["h"][:], ACT.Identity, bias=neg_s[:], scale=2.0)
            nc.scalar.activation(split(d["tn"][:]), d["a"], ACT.Tanh, scale=half_s[:])

        def s_base(hf):
            st[hf]["bs"] = keep.tile([P, PAIRS, RUN], F32, name="bs%d" % hf, tag="zs_ps%d_turned" % hf, align_bytes=64)
            nc.scalar.copy(out=split(st[hf]["bs"][:]), in_=dealt(base_sb[:, hf * JH : (hf + 1) * JH]))

        def v_ph(hf):
            d = st[hf]
            nc.vector.tensor_tensor(d["pp"][:, :, 1, :], d["p"], d["h"][:], ALU.mult)
            d["zs_ps"] = turn_sums("zs_ps%d" % hf, hf, d["pp"])

        def back_zs(hf):
            st[hf]["zs"] = turn_back("zs_ps%d" % hf, st[hf]["zs_ps"])

        def back_aa(hf):
            st[hf]["sums"] = turn_back("aa_ps%d" % hf, st[hf]["aa_ps"])

        def v_rz(hf):
            d = st[hf]
            d["rz"] = keep.tile([P, GH], F32, name="rz%d" % hf, tag=("rz0", "d0")[hf])
            nc.vector.reciprocal(d["rz"][:], d["zs"][:, 0, :])

        def v_m(hf):
            d = st[hf]
            nc.vector.tensor_tensor(d["m"][:], d["zs"][:, 1, :], d["rz"][:], ALU.mult)

        def v_x(hf):
            d = st[hf]
            nc.vector.scalar_tensor_tensor(d["xy"][:, :, 0, :], d["p"], s_col[:], d["pn"][:], ALU.mult, ALU.mult)

        def v_npu(hf):
            d = st[hf]
            nc.vector.scalar_tensor_tensor(d["npu"][:], d["h2"][:], 1.0, d["p"], ALU.subtract, ALU.mult)

        def v_d(hf):
            d = st[hf]
            d["d"] = keep.tile([P, PAIRS, RUN], F32, name="d%d" % hf, tag="d%d" % hf)
            nc.vector.tensor_tensor(split(d["d"][:]), split(d["h"][:]), spread(d["m"][:]), ALU.subtract)

        def v_xd(hf):
            d = st[hf]
            d["xd"] = keep.tile([P, PAIRS, RUN], F32, name="xd%d" % hf, tag="xd%d" % hf)
            nc.vector.tensor_tensor(d["xd"][:], d["xy"][:, :, 0, :], d["d"][:], ALU.mult)

        def v_y(hf):
            d = st[hf]
            nc.vector.tensor_tensor(d["xy"][:, :, 1, :], d["xd"][:], d["npu"][:], ALU.subtract)

        def v_ds(hf):
            st[hf]["ds_g"] = gather("ds_g", ds, U8, hf)

        def v_dw(hf):
            st[hf]["t"] = product("t%d" % hf, w1_q, gather("dw_g", dw, U32, hf), st[hf]["ds_g"])

        def v_e(hf):
            d = st[hf]
            nc.vector.scalar_tensor_tensor(d["e"][:], c0[:, hf * GH : (hf + 1) * GH], og_col[:], d["rz"][:], ALU.mult, ALU.mult)

        def v_te(hf):
            d = st[hf]
            nc.vector.tensor_tensor(split(d["te"][:]), dealt(d["t"][:]), spread(d["e"][:]), ALU.mult)

        def v_aa(hf):
            d = st[hf]
            nc.vector.tensor_tensor(d["aa"][:], d["xy"][:], d["te"][:].unsqueeze(2).to_broadcast([P, PAIRS, 2, RUN]), ALU.mult)

        def pe_sums(hf):
            st[hf]["aa_ps"] = turn_sums("aa_ps%d" % hf, hf, st[hf]["aa"])

        def v_sums(hf):
            d = st[hf]
            sums = keep.tile([P, 2 * GH], F32, name="sums%d" % hf)
            nc.vector.tensor_reduce(sums[:], d["aa"][:].rearrange("p i q (g e) -> p (q g) i e", e=2), AX.XY, ALU.add)
            d["sums"] = sums[:].rearrange("p (q g) -> p q g", q=2)

        def v_am(hf):
            d = st[hf]
            nc.vector.scalar_tensor_tensor(d["am"][:], d["sums"][:, ::-1, :], -1.0,
                                           d["rz"][:].unsqueeze(1).to_broadcast([P, 2, GH]), ALU.mult, ALU.mult)

        def v_pm(hf):
            d = st[hf]
            d["pm"] = keep.tile([P, PAIRS, RUN], F32, name="pm%d" % hf, tag=("xd1", "d1")[hf])
            nc.vector.tensor_tensor(d["pm"][:], d["npu"][:], d["m2"][:], ALU.mult)

        def v_u1(hf):
            d = st[hf]
            nc.vector.tensor_tensor(d["u1"][:], d["te"][:], d["pm"][:], ALU.mult)

        def v_u2(hf):
            d = st[hf]
            nc.vector.scalar_tensor_tensor(d["u2"][:], d["aa"][:, :, 1, :], neg_s[:], d["tn"][:], ALU.mult, ALU.mult)

        def v_bb(hf):
            d = st[hf]
            for q in range(2):
                nc.vector.tensor_tensor(split(d["bb"][:, q, :, :]), split(d["xy"][:, :, q, :]), spread(d["am"][:, q, :]), ALU.mult)

        def add_terms(hf, terms, tags):
            banks = [psum.tile([P, P], F32, name="u_ps%d%d" % (hf, c), tag=tags[c]) for c in range(2)]
            for n, term in enumerate(terms):
                for c in range(2):
                    nc.tensor.matmul(banks[c][:], lhsT=term[:, 2 * c : 2 * c + 2, :].rearrange("p i x -> p (i x)"), rhs=ident[:],
                                     start=(n == 0), stop=(n == len(terms) - 1), is_transpose=True)
            back = psum.tile([P, 2, P], F32, name="u_back%d" % hf, tag=tags[2])
            for c in range(2):
                turned = keep.tile([P, P], F32, name="u_turned%d%d" % (hf, c))
                nc.scalar.copy(out=turned[:], in_=banks[c][:])
                nc.tensor.transpose(back[:, c, :], turned[:], ident[:])
            return back[:].rearrange("p c (j g e) -> p g (c j) e", j=2, e=2)

        def store(hf, y):
            nc.sync.dma_start(out=out[:, hf * JH : (hf + 1) * JH], in_=y[:].rearrange("p g i e -> p (g i e)"))

        wo_q = quantise("wo", wo_raw)
        base_sb = keep.tile([P, J], F32, name="base_sb", tag="wo_raw")
        nc.sync.dma_start(out=base_sb[:], in_=base)
        dy_q = quantise("dy", dy_raw)
        og_col = keep.tile([P, 1], F32, name="og_col", tag="dy_raw")
        nc.sync.dma_start(out=og_col[:], in_=og)
        c0 = product("c0", wo_q, dy_q[0], dy_q[1])
        s_ph(0)
        s_ph(1)
        v_ds(0)
        v_ds(1)
        v_ph(0)
        v_ph(1)
        s_pn_h2(0)
        back_zs(0)
        s_pn_h2(1)
        back_zs(1)
        v_x(0)
        v_npu(0)
        v_dw(0)
        v_dw(1)
        v_x(1)
        v_npu(1)
        v_rz(0)
        s_rest(0)
        s_rest(1)
        s_base(0)
        s_base(1)
        v_m(0)
        v_e(0)
        v_d(0)
        v_te(0)
        v_xd(0)
        v_rz(1)
        v_y(0)
        v_m(1)
        v_aa(0)
        pe_sums(0)
        back_aa(0)
        v_d(1)
        v_e(1)
        v_xd(1)
        v_te(1)
        v_y(1)
        v_pm(0)
        v_u2(0)
        v_u1(0)
        v_am(0)
        v_pm(1)
        v_bb(0)
        d = st[0]
        whole0 = add_terms(0, (d["bs"], d["u1"], d["u2"], d["bb"][:, 0, :, :], d["bb"][:, 1, :, :]), ("a0", "t0", "spare"))
        y0 = keep.tile([P, GH, PAIRS, 2], F32, name="y0")
        nc.scalar.copy(out=y0[:], in_=whole0)
        store(0, y0)
        v_u1(1)
        v_aa(1)
        v_u2(1)
        d = st[1]
        part1 = add_terms(1, (d["bs"], d["u1"], d["u2"]), ("a1", "t1", "c0"))
        v_sums(1)
        v_am(1)
        v_bb(1)
        d = st[1]
        u4 = wide("u4", 1)
        nc.vector.tensor_tensor(u4[:], d["bb"][:, 0, :, :], d["bb"][:, 1, :, :], ALU.add)
        y1 = keep.tile([P, GH, PAIRS, 2], F32, name="y1")
        nc.vector.tensor_tensor(y1[:], part1, u4[:].rearrange("p i (g e) -> p g i e", e=2), ALU.add)
        store(1, y1)
